import numpy as np
import ml_dtypes


def mxq(x, axis, fmt="e4m3"):
    dtype, down = {"e4m3": (ml_dtypes.float8_e4m3fn, 7), "e5m2": (ml_dtypes.float8_e5m2, 14)}[fmt]
    v = np.moveaxis(np.asarray(x, np.float32).astype(ml_dtypes.bfloat16).astype(np.float64), axis, -1)
    blocks = v.reshape(v.shape[:-1] + (-1, 32))
    amax = np.abs(blocks).max(-1, keepdims=True)
    byte = np.maximum(np.where(amax > 0, np.frexp(amax)[1] - 1 + 127, 0) - down, 1)
    scale = np.exp2(byte - 127.0)
    codes = (blocks / scale).astype(np.float32).astype(dtype).astype(np.float64)
    return np.moveaxis((codes * scale).reshape(v.shape), -1, axis)


WIDE = False


def mx_kscale(k, group=512):
    if not WIDE:
        return np.ones(k)
    levels = np.array([18, -18])
    if group != 512:
        return np.exp2(np.random.permutation(np.resize(levels, k // group))).repeat(group)
    if k % 512:
        return np.exp2(np.random.permutation(np.resize(levels, k // 32))).repeat(32)
    a = np.empty((k // 512, 16))
    for p in range(k // 512):
        a[p, :8] = np.random.permutation(np.resize(levels, 8))
        for g in range(8):
            far = levels[np.abs(levels - a[p, g]) >= 10]
            a[p, g + 8] = far[np.random.randint(len(far))]
    return np.exp2(a.ravel()).repeat(32)


def f64(x):
    return np.asarray(x).astype(np.float64)


def sigmoid(v):
    return 1.0 / (1.0 + np.exp(-v))


G, D, M, N = 4, 128, 128, 512


def setup_inputs():
    n = np.random.standard_normal
    s_d = mx_kscale(D, 0)
    return {
        "x": (n((G, D, N)) * s_d[:, None]).astype(np.float32),
        "w1": (n((G, D, M)) / np.sqrt(D) / s_d[:, None]).astype(np.float32),
        "w2": (n((G, D, M)) / np.sqrt(D) / s_d[:, None]).astype(np.float32),
        "th": (np.random.uniform(0.5, 1.5, (G, M, 1))).astype(np.float32),
        "dx": (n((G, D, N)) * s_d[:, None]).astype(np.float32),
        "og": (np.random.uniform(0.5, 2.0, (G, M, 1))).astype(np.float32),
        "base": (0.3 * n((G, M, N))).astype(np.float32),
    }


def reference(x, w1, w2, th, dx, og, base):
    w1q = mxq(f64(w1), 1, "e4m3")
    xq = mxq(f64(x), 1, "e4m3")
    z1 = w1q.transpose(0, 2, 1) @ xq
    dxq = mxq(f64(dx), 1, "e4m3")
    tz1 = w1q.transpose(0, 2, 1) @ dxq
    w2q = mxq(f64(w2), 1, "e4m3")
    z2 = w2q.transpose(0, 2, 1) @ xq
    tz2 = w2q.transpose(0, 2, 1) @ dxq
    mg = np.sqrt(np.square(z1) + np.square(z2) + 0.05)
    xmg = (tz1 * z1 * 2.0 + tz2 * z2 * 2.0) * 0.5 / mg
    xh = xmg * sigmoid(mg - f64(th)) + xmg * sigmoid(mg - f64(th)) * (1.0 - sigmoid(mg - f64(th))) * mg
    y = xh * f64(og) + f64(base)
    return y

@@ -1,0 +1,233 @@
+from contextlib import ExitStack
+
+import concourse.mybir as mybir
+
+G, D, M, N = 4, 128, 128, 512
+FLOPS = 4 * 2 * G * D * M * N
+
+F32 = mybir.dt.float32
+BF16 = mybir.dt.bfloat16
+U32 = mybir.dt.uint32
+U8 = mybir.dt.uint8
+FP8X4 = mybir.dt.float8_e4m3fn_x4
+ACT = mybir.ActivationFunctionType
+ALU = mybir.AluOpType
+
+P = 128
+PACK = 4
+ROWS = D // PACK
+MM_N = 128
+FLOOR = 0.05
+CHUNKS = [(0, 128), (128, 256), (384, 128)]
+BANK_COLS = 256
+
+
+def tile_rows_tnmagnitude_kernel(tc, x, w1, w2, th, dx, og, base, out):
+    nc = tc.nc
+    with ExitStack() as ctx:
+        sb = ctx.enter_context(tc.tile_pool(name="sb", bufs=1))
+        ps = ctx.enter_context(tc.psum_pool(name="ps", bufs=1))
+        ctx.enter_context(tc.manual_schedule())
+
+        def operand(name, width):
+            raw = sb.tile([P, PACK, width], F32, name=name + "_raw")
+            packed = sb.tile([P, width * PACK], BF16, name=name + "_bf", align_bytes=64)
+            codes = sb.tile([P, width], U32, name=name + "_codes", align_bytes=64)
+            scales = sb.tile([P, width], U8, name=name + "_scales", align_bytes=64)
+            return raw, packed, codes, scales
+
+        w_op = [operand("w%d" % i, M) for i in range(2)]
+        x_op = [operand("x%d" % c, CHUNKS[c][1]) for c in range(len(CHUNKS))]
+        dx_op = [operand("dx%d" % c, CHUNKS[c][1]) for c in range(len(CHUNKS))]
+
+        def load(op, src, c0, width):
+            nc.sync.dma_start(out=op[0][:], in_=src.rearrange("g (p j) n -> (g p) j n", j=PACK)[:, :, c0 : c0 + width])
+
+        base_sb = sb.tile([P, G, N], F32, name="base_sb")
+        th_sb = sb.tile([P, G], F32, name="th_sb")
+        og_sb = sb.tile([P, G], F32, name="og_sb")
+        load(x_op[0], x, *CHUNKS[0])
+        load(w_op[0], w1, 0, M)
+        load(w_op[1], w2, 0, M)
+        load(x_op[1], x, *CHUNKS[1])
+        load(dx_op[0], dx, *CHUNKS[0])
+        load(x_op[2], x, *CHUNKS[2])
+        load(dx_op[1], dx, *CHUNKS[1])
+        load(dx_op[2], dx, *CHUNKS[2])
+        nc.sync.dma_start(out=base_sb[:], in_=base.rearrange("g m n -> m g n"))
+        with nc.allow_non_contiguous_dma(reason="one value a partition and group"):
+            nc.sync.dma_start(out=th_sb[:], in_=th.rearrange("g m o -> m (g o)"))
+            nc.sync.dma_start(out=og_sb[:], in_=og.rearrange("g m o -> m (g o)"))
+
+        two = sb.tile([P, 1], F32, name="two")
+        ln2 = sb.tile([P, 1], F32, name="ln2")
+        nc.gpsimd.memset(two[:], 2.0)
+        nc.scalar.activation(out=ln2[:], in_=two[:], func=ACT.Ln)
+        th_bias = sb.tile([P, G], F32, name="th_bias")
+
+        def interleave(copy, op):
+            copy(
+                out=op[1][:].rearrange("p (c i t) -> p c t i", i=4, t=PACK),
+                in_=op[0][:].rearrange("p t (c i) -> p c t i", i=4),
+            )
+
+        def quantize(op):
+            nc.vector.quantize_mx(out=op[2][:].bitcast(FP8X4), scales=op[3][:], in_=op[1][:])
+
+        z_bank = [ps.tile([P, 2, BANK_COLS], F32, name="z_bank%d" % g) for g in range(G)]
+        tz_bank = [ps.tile([P, 2, BANK_COLS], F32, name="tz_bank%d" % g) for g in range(G)]
+
+        def product(bank, op, c, g, part):
+            rows = slice(ROWS * g, ROWS * (g + 1))
+            for c0 in range(0, CHUNKS[c][1], MM_N):
+                cols = slice(c0, c0 + MM_N)
+                nc.tensor.matmul_mx(
+                    out=bank[g][:, part, cols],
+                    lhsT=w_op[part][2][rows, :].bitcast(FP8X4),
+                    lhsT_scale=w_op[part][3][rows, :],
+                    rhs=op[c][2][rows, cols].bitcast(FP8X4),
+                    rhs_scale=op[c][3][rows, cols],
+                    start=True,
+                    stop=True,
+                )
+
+        def products(bank, op, c):
+            for g in range(G):
+                for part in range(2):
+                    product(bank, op, c, g, part)
+
+        nch = len(CHUNKS)
+        z = [[sb.tile([P, 2, CHUNKS[c][1]], F32, name="z%d_%d" % (c, g)) for g in range(G)] for c in range(nch)]
+        zsq = [sb.tile([P, G, 2, CHUNKS[c][1]], F32, name="zsq%d" % c) for c in range(nch)]
+        prod = [sb.tile([P, G, 2, CHUNKS[c][1]], F32, name="prod%d" % c) for c in range(nch)]
+        ssum = [sb.tile([P, G, CHUNKS[c][1]], F32, name="ssum%d" % c) for c in range(nch)]
+        logs = sb.tile([P, G, N], F32, name="logs")
+        dot = sb.tile([P, G, N], F32, name="dot")
+        vcopy = nc.vector.tensor_copy
+        scopy = nc.scalar.copy
+
+        def span(c):
+            return slice(CHUNKS[c][0], CHUNKS[c][0] + CHUNKS[c][1])
+
+        def copy_z(copy, c, g):
+            copy(out=z[c][g][:], in_=z_bank[g][:, :, : CHUNKS[c][1]])
+
+        def square_z(c, g):
+            nc.scalar.activation(out=zsq[c][:, g, :, :], in_=z_bank[g][:, :, : CHUNKS[c][1]], func=ACT.Square)
+
+        def square_copy(c, g):
+            nc.scalar.activation(out=zsq[c][:, g, :, :], in_=z[c][g][:], func=ACT.Square)
+
+        def sum_squares(c, g0, g1):
+            nc.vector.scalar_tensor_tensor(
+                out=ssum[c][:, g0:g1, :], in0=zsq[c][:, g0:g1, 0, :], scalar=FLOOR, in1=zsq[c][:, g0:g1, 1, :], op0=ALU.add, op1=ALU.add
+            )
+
+        def multiply(c, g):
+            nc.vector.scalar_tensor_tensor(
+                out=prod[c][:, g, :, :], in0=tz_bank[g][:, :, : CHUNKS[c][1]], scalar=0.25, in1=z[c][g][:], op0=ALU.mult, op1=ALU.mult
+            )
+
+        def add_products(eng, c, g0, g1):
+            eng.tensor_tensor(out=dot[:, g0:g1, span(c)], in0=prod[c][:, g0:g1, 0, :], in1=prod[c][:, g0:g1, 1, :], op=ALU.add)
+
+        def take_log(c, g0, g1):
+            nc.scalar.activation(out=logs[:, g0:g1, span(c)], in_=ssum[c][:, g0:g1, :], func=ACT.Ln)
+
+        interleave(vcopy, x_op[0])
+        interleave(scopy, w_op[0])
+        quantize(x_op[0])
+        interleave(vcopy, w_op[1])
+        quantize(w_op[0])
+        quantize(w_op[1])
+        for part in range(2):
+            for g in range(G):
+                product(z_bank, x_op, 0, g, part)
+        for g in range(G):
+            square_z(0, g)
+            copy_z(scopy, 0, g)
+        interleave(vcopy, x_op[1])
+        interleave(vcopy, dx_op[0])
+        quantize(x_op[1])
+        quantize(dx_op[0])
+        for g in range(G):
+            for part in range(2):
+                product(tz_bank, dx_op, 0, g, part)
+            for part in range(2):
+                product(z_bank, x_op, 1, g, part)
+        interleave(vcopy, x_op[2])
+        multiply(0, 0)
+        quantize(x_op[2])
+        interleave(vcopy, dx_op[1])
+        multiply(0, 1)
+        multiply(0, 2)
+        quantize(dx_op[1])
+        multiply(0, 3)
+        products(tz_bank, dx_op, 1)
+        for g in range(G):
+            square_z(1, g)
+            if g < 3:
+                copy_z(scopy, 1, g)
+        interleave(vcopy, dx_op[2])
+        sum_squares(0, 0, G)
+        quantize(dx_op[2])
+        take_log(0, 0, G)
+        add_products(nc.vector, 0, 0, G)
+        multiply(1, 0)
+        multiply(1, 1)
+        copy_z(vcopy, 1, 3)
+        products(z_bank, x_op, 2)
+        multiply(1, 2)
+        sum_squares(1, 0, G)
+        multiply(1, 3)
+        products(tz_bank, dx_op, 2)
+        for g in range(G):
+            square_z(2, g)
+            copy_z(scopy, 2, g)
+        nc.scalar.mul(out=th_bias[:], in_=th_sb[:], mul=-0.5)
+        take_log(1, 0, G)
+        sum_squares(2, 0, G)
+        take_log(2, 0, G)
+        multiply(2, 0)
+        multiply(2, 1)
+        add_products(nc.vector, 1, 0, G)
+        multiply(2, 2)
+        multiply(2, 3)
+        add_products(nc.vector, 2, 0, G)
+
+        pieces = [(0, 0, 256), (0, 256, 256), (1, 0, 512), (2, 0, 512), (3, 0, 256), (3, 256, 256)]
+        scaled = {}
+
+        def gate(i):
+            g, c0, width = pieces[i]
+            cols = slice(c0, c0 + width)
+            mag = sb.tile([P, width], F32, name="mag%d" % i)
+            inv2 = sb.tile([P, width], F32, name="inv2_%d" % i)
+            tnh = sb.tile([P, width], F32, name="tnh%d" % i)
+            nc.scalar.activation(out=mag[:], in_=logs[:, g, cols], func=ACT.Exp, scale=0.5)
+            nc.scalar.activation(out=inv2[:], in_=logs[:, g, cols], func=ACT.Exp, scale=-0.5, bias=ln2[:])
+            nc.scalar.activation(out=tnh[:], in_=mag[:], func=ACT.Tanh, scale=0.5, bias=th_bias[:, g : g + 1])
+            return inv2, tnh
+
+        def finish(i):
+            g, c0, width = pieces[i]
+            cols = slice(c0, c0 + width)
+            res = sb.tile([P, width], F32, name="res%d" % i)
+            nc.vector.tensor_tensor(out=res[:], in0=scaled[i][:], in1=base_sb[:, g, cols], op=ALU.add)
+            nc.sync.dma_start(out=out[g, :, cols], in_=res[:])
+
+        for i in range(len(pieces)):
+            g, c0, width = pieces[i]
+            cols = slice(c0, c0 + width)
+            inv2, tnh = gate(i)
+            slope = sb.tile([P, width], F32, name="slope%d" % i)
+            gated = sb.tile([P, width], F32, name="gated%d" % i)
+            scaled[i] = sb.tile([P, width], F32, name="scaled%d" % i)
+            nc.vector.scalar_tensor_tensor(out=slope[:], in0=inv2[:], scalar=1.0, in1=tnh[:], op0=ALU.add, op1=ALU.subtract)
+            nc.vector.scalar_tensor_tensor(out=gated[:], in0=tnh[:], scalar=1.0, in1=dot[:, g, cols], op0=ALU.add, op1=ALU.mult)
+            if i > 0:
+                finish(i - 1)
+            nc.vector.scalar_tensor_tensor(
+                out=scaled[i][:], in0=gated[:], scalar=og_sb[:, g : g + 1], in1=slope[:], op0=ALU.mult, op1=ALU.mult
+            )
+        finish(len(pieces) - 1)

@@ -46,8 +46,8 @@ def tile_rows_tnmagnitude_kernel(tc, x, w1, w2, th, dx, og, base, out):
         base_sb = sb.tile([P, G, N], F32, name="base_sb")
         th_sb = sb.tile([P, G], F32, name="th_sb")
         og_sb = sb.tile([P, G], F32, name="og_sb")
-        load(x_op[0], x, *CHUNKS[0])
         load(w_op[0], w1, 0, M)
+        load(x_op[0], x, *CHUNKS[0])
         load(w_op[1], w2, 0, M)
         load(x_op[1], x, *CHUNKS[1])
         load(dx_op[0], dx, *CHUNKS[0])
@@ -63,6 +63,8 @@ def tile_rows_tnmagnitude_kernel(tc, x, w1, w2, th, dx, og, base, out):
         ln2 = sb.tile([P, 1], F32, name="ln2")
         nc.gpsimd.memset(two[:], 2.0)
         nc.scalar.activation(out=ln2[:], in_=two[:], func=ACT.Ln)
+        floor = sb.tile([P, 1], F32, name="floor")
+        nc.scalar.mul(out=floor[:], in_=two[:], mul=FLOOR / 2.0)
         th_bias = sb.tile([P, G], F32, name="th_bias")
 
         def interleave(copy, op):
@@ -77,27 +79,24 @@ def tile_rows_tnmagnitude_kernel(tc, x, w1, w2, th, dx, og, base, out):
         z_bank = [ps.tile([P, 2, BANK_COLS], F32, name="z_bank%d" % g) for g in range(G)]
         tz_bank = [ps.tile([P, 2, BANK_COLS], F32, name="tz_bank%d" % g) for g in range(G)]
 
-        def product(bank, op, c, g, part):
-            rows = slice(ROWS * g, ROWS * (g + 1))
-            for c0 in range(0, CHUNKS[c][1], MM_N):
-                cols = slice(c0, c0 + MM_N)
-                nc.tensor.matmul_mx(
-                    out=bank[g][:, part, cols],
-                    lhsT=w_op[part][2][rows, :].bitcast(FP8X4),
-                    lhsT_scale=w_op[part][3][rows, :],
-                    rhs=op[c][2][rows, cols].bitcast(FP8X4),
-                    rhs_scale=op[c][3][rows, cols],
-                    start=True,
-                    stop=True,
-                )
-
-        def products(bank, op, c):
-            for g in range(G):
-                for part in range(2):
-                    product(bank, op, c, g, part)
+        def products(bank, op, c, groups, parts=(0, 1)):
+            for part in parts:
+                for c0 in range(0, CHUNKS[c][1], MM_N):
+                    cols = slice(c0, c0 + MM_N)
+                    for g in groups:
+                        rows = slice(ROWS * g, ROWS * (g + 1))
+                        nc.tensor.matmul_mx(
+                            out=bank[g][:, part, cols],
+                            lhsT=w_op[part][2][rows, :].bitcast(FP8X4),
+                            lhsT_scale=w_op[part][3][rows, :],
+                            rhs=op[c][2][rows, cols].bitcast(FP8X4),
+                            rhs_scale=op[c][3][rows, cols],
+                            start=True,
+                            stop=True,
+                        )
 
         nch = len(CHUNKS)
-        z = [[sb.tile([P, 2, CHUNKS[c][1]], F32, name="z%d_%d" % (c, g)) for g in range(G)] for c in range(nch)]
+        z = [sb.tile([P, G, 2, CHUNKS[c][1]], F32, name="z%d" % c) for c in range(nch)]
         zsq = [sb.tile([P, G, 2, CHUNKS[c][1]], F32, name="zsq%d" % c) for c in range(nch)]
         prod = [sb.tile([P, G, 2, CHUNKS[c][1]], F32, name="prod%d" % c) for c in range(nch)]
         ssum = [sb.tile([P, G, CHUNKS[c][1]], F32, name="ssum%d" % c) for c in range(nch)]
@@ -110,92 +109,103 @@ def tile_rows_tnmagnitude_kernel(tc, x, w1, w2, th, dx, og, base, out):
             return slice(CHUNKS[c][0], CHUNKS[c][0] + CHUNKS[c][1])
 
         def copy_z(copy, c, g):
-            copy(out=z[c][g][:], in_=z_bank[g][:, :, : CHUNKS[c][1]])
+            copy(out=z[c][:, g, :, :], in_=z_bank[g][:, :, : CHUNKS[c][1]])
+
+        def copy_part(copy, c, g, part):
+            copy(out=z[c][:, g, part, :], in_=z_bank[g][:, part, : CHUNKS[c][1]])
 
         def square_z(c, g):
             nc.scalar.activation(out=zsq[c][:, g, :, :], in_=z_bank[g][:, :, : CHUNKS[c][1]], func=ACT.Square)
 
-        def square_copy(c, g):
-            nc.scalar.activation(out=zsq[c][:, g, :, :], in_=z[c][g][:], func=ACT.Square)
+        def square_copy(c, g0, g1):
+            nc.scalar.activation(out=zsq[c][:, g0:g1, :, :], in_=z[c][:, g0:g1, :, :], func=ACT.Square)
 
-        def sum_squares(c, g0, g1):
-            nc.vector.scalar_tensor_tensor(
-                out=ssum[c][:, g0:g1, :], in0=zsq[c][:, g0:g1, 0, :], scalar=FLOOR, in1=zsq[c][:, g0:g1, 1, :], op0=ALU.add, op1=ALU.add
-            )
+        def square_part(c, part):
+            nc.scalar.activation(out=zsq[c][:, :, part, :], in_=z[c][:, :, part, :], func=ACT.Square)
+
+        def sum_squares(eng, c, g0, g1):
+            eng.tensor_tensor(out=ssum[c][:, g0:g1, :], in0=zsq[c][:, g0:g1, 0, :], in1=zsq[c][:, g0:g1, 1, :], op=ALU.add)
 
         def multiply(c, g):
             nc.vector.scalar_tensor_tensor(
-                out=prod[c][:, g, :, :], in0=tz_bank[g][:, :, : CHUNKS[c][1]], scalar=0.25, in1=z[c][g][:], op0=ALU.mult, op1=ALU.mult
+                out=prod[c][:, g, :, :], in0=tz_bank[g][:, :, : CHUNKS[c][1]], scalar=0.25, in1=z[c][:, g, :, :], op0=ALU.mult, op1=ALU.mult
             )
 
         def add_products(eng, c, g0, g1):
             eng.tensor_tensor(out=dot[:, g0:g1, span(c)], in0=prod[c][:, g0:g1, 0, :], in1=prod[c][:, g0:g1, 1, :], op=ALU.add)
 
         def take_log(c, g0, g1):
-            nc.scalar.activation(out=logs[:, g0:g1, span(c)], in_=ssum[c][:, g0:g1, :], func=ACT.Ln)
+            nc.scalar.activation(out=logs[:, g0:g1, span(c)], in_=ssum[c][:, g0:g1, :], func=ACT.Ln, bias=floor[:])
 
+        ALL = range(G)
+        interleave(vcopy, w_op[0])
         interleave(vcopy, x_op[0])
-        interleave(scopy, w_op[0])
-        quantize(x_op[0])
-        interleave(vcopy, w_op[1])
         quantize(w_op[0])
-        quantize(w_op[1])
-        for part in range(2):
-            for g in range(G):
-                product(z_bank, x_op, 0, g, part)
+        quantize(x_op[0])
+        products(z_bank, x_op, 0, ALL, (0,))
         for g in range(G):
-            square_z(0, g)
-            copy_z(scopy, 0, g)
+            copy_part(scopy, 0, g, 0)
+        interleave(vcopy, w_op[1])
+        quantize(w_op[1])
+        products(z_bank, x_op, 0, ALL, (1,))
+        for g in range(G):
+            copy_part(scopy, 0, g, 1)
+        square_part(0, 0)
+        square_part(0, 1)
         interleave(vcopy, x_op[1])
         interleave(vcopy, dx_op[0])
         quantize(x_op[1])
         quantize(dx_op[0])
-        for g in range(G):
-            for part in range(2):
-                product(tz_bank, dx_op, 0, g, part)
-            for part in range(2):
-                product(z_bank, x_op, 1, g, part)
+        products(z_bank, x_op, 1, ALL)
+        products(tz_bank, dx_op, 0, ALL)
         interleave(vcopy, x_op[2])
-        multiply(0, 0)
+
+        sum_squares(nc.gpsimd, 0, 0, G)
         quantize(x_op[2])
-        interleave(vcopy, dx_op[1])
-        multiply(0, 1)
-        multiply(0, 2)
-        quantize(dx_op[1])
-        multiply(0, 3)
-        products(tz_bank, dx_op, 1)
         for g in range(G):
-            square_z(1, g)
-            if g < 3:
-                copy_z(scopy, 1, g)
+            multiply(0, g)
+        interleave(vcopy, dx_op[1])
+        add_products(nc.gpsimd, 0, 0, G)
+        copy_z(scopy, 1, 0)
+        copy_z(scopy, 1, 1)
+        products(z_bank, x_op, 2, (0, 1))
+        copy_z(scopy, 1, 2)
+        square_z(1, 3)
+        copy_z(vcopy, 2, 0)
+        copy_z(vcopy, 2, 1)
+        copy_z(vcopy, 1, 3)
+        products(z_bank, x_op, 2, (2, 3))
+        quantize(dx_op[1])
+        products(tz_bank, dx_op, 1, ALL)
         interleave(vcopy, dx_op[2])
-        sum_squares(0, 0, G)
+        square_copy(1, 0, 3)
+        square_copy(2, 0, 2)
+        square_z(2, 2)
+        square_z(2, 3)
+        sum_squares(nc.vector, 1, 0, G)
         quantize(dx_op[2])
+        sum_squares(nc.vector, 2, 0, G)
+        nc.scalar.mul(out=th_bias[:], in_=th_sb[:], mul=-0.5)
         take_log(0, 0, G)
-        add_products(nc.vector, 0, 0, G)
+        take_log(1, 0, G)
+        take_log(2, 0, G)
         multiply(1, 0)
         multiply(1, 1)
-        copy_z(vcopy, 1, 3)
-        products(z_bank, x_op, 2)
+        add_products(nc.gpsimd, 1, 0, 2)
+        products(tz_bank, dx_op, 2, (0, 1))
         multiply(1, 2)
-        sum_squares(1, 0, G)
         multiply(1, 3)
-        products(tz_bank, dx_op, 2)
-        for g in range(G):
-            square_z(2, g)
-            copy_z(scopy, 2, g)
-        nc.scalar.mul(out=th_bias[:], in_=th_sb[:], mul=-0.5)
-        take_log(1, 0, G)
-        sum_squares(2, 0, G)
-        take_log(2, 0, G)
+        products(tz_bank, dx_op, 2, (2, 3))
+        add_products(nc.gpsimd, 1, 2, 4)
+        copy_z(vcopy, 2, 2)
+        copy_z(vcopy, 2, 3)
         multiply(2, 0)
         multiply(2, 1)
-        add_products(nc.vector, 1, 0, G)
         multiply(2, 2)
         multiply(2, 3)
-        add_products(nc.vector, 2, 0, G)
+        add_products(nc.vector, 2, 0, 2)
 
-        pieces = [(0, 0, 256), (0, 256, 256), (1, 0, 512), (2, 0, 512), (3, 0, 256), (3, 256, 256)]
+        pieces = [(0, 0, 256), (0, 256, 256), (1, 0, 256), (1, 256, 256), (2, 0, 512), (3, 0, 384), (3, 384, 128)]
         scaled = {}
 
         def gate(i):
@@ -227,6 +237,8 @@ def tile_rows_tnmagnitude_kernel(tc, x, w1, w2, th, dx, og, base, out):
             nc.vector.scalar_tensor_tensor(out=gated[:], in0=tnh[:], scalar=1.0, in1=dot[:, g, cols], op0=ALU.add, op1=ALU.mult)
             if i > 0:
                 finish(i - 1)
+            else:
+                add_products(nc.vector, 2, 2, 4)
             nc.vector.scalar_tensor_tensor(
                 out=scaled[i][:], in0=gated[:], scalar=og_sb[:, g : g + 1], in1=slope[:], op0=ALU.mult, op1=ALU.mult
             )

@@ -18,7 +18,7 @@ PACK = 4
 ROWS = D // PACK
 MM_N = 128
 FLOOR = 0.05
-CHUNKS = [(0, 128), (128, 256), (384, 128)]
+CHUNKS = [(0, 128), (128, 128), (256, 256)]
 BANK_COLS = 256
 
 
@@ -49,8 +49,8 @@ def tile_rows_tnmagnitude_kernel(tc, x, w1, w2, th, dx, og, base, out):
         load(w_op[0], w1, 0, M)
         load(x_op[0], x, *CHUNKS[0])
         load(w_op[1], w2, 0, M)
-        load(x_op[1], x, *CHUNKS[1])
         load(dx_op[0], dx, *CHUNKS[0])
+        load(x_op[1], x, *CHUNKS[1])
         load(x_op[2], x, *CHUNKS[2])
         load(dx_op[1], dx, *CHUNKS[1])
         load(dx_op[2], dx, *CHUNKS[2])
@@ -98,7 +98,7 @@ def tile_rows_tnmagnitude_kernel(tc, x, w1, w2, th, dx, og, base, out):
         nch = len(CHUNKS)
         z = [sb.tile([P, G, 2, CHUNKS[c][1]], F32, name="z%d" % c) for c in range(nch)]
         zsq = [sb.tile([P, G, 2, CHUNKS[c][1]], F32, name="zsq%d" % c) for c in range(nch)]
-        prod = [sb.tile([P, G, 2, CHUNKS[c][1]], F32, name="prod%d" % c) for c in range(nch)]
+        prod = sb.tile([P, G, 2, N], F32, name="prod")
         ssum = [sb.tile([P, G, CHUNKS[c][1]], F32, name="ssum%d" % c) for c in range(nch)]
         logs = sb.tile([P, G, N], F32, name="logs")
         dot = sb.tile([P, G, N], F32, name="dot")
@@ -128,11 +128,11 @@ def tile_rows_tnmagnitude_kernel(tc, x, w1, w2, th, dx, og, base, out):
 
         def multiply(c, g):
             nc.vector.scalar_tensor_tensor(
-                out=prod[c][:, g, :, :], in0=tz_bank[g][:, :, : CHUNKS[c][1]], scalar=0.25, in1=z[c][:, g, :, :], op0=ALU.mult, op1=ALU.mult
+                out=prod[:, g, :, span(c)], in0=tz_bank[g][:, :, : CHUNKS[c][1]], scalar=0.25, in1=z[c][:, g, :, :], op0=ALU.mult, op1=ALU.mult
             )
 
-        def add_products(eng, c, g0, g1):
-            eng.tensor_tensor(out=dot[:, g0:g1, span(c)], in0=prod[c][:, g0:g1, 0, :], in1=prod[c][:, g0:g1, 1, :], op=ALU.add)
+        def add_products(eng, c0, c1, g0, g1):
+            eng.tensor_tensor(out=dot[:, g0:g1, c0:c1], in0=prod[:, g0:g1, 0, c0:c1], in1=prod[:, g0:g1, 1, c0:c1], op=ALU.add)
 
         def take_log(c, g0, g1):
             nc.scalar.activation(out=logs[:, g0:g1, span(c)], in_=ssum[c][:, g0:g1, :], func=ACT.Ln, bias=floor[:])
@@ -151,61 +151,58 @@ def tile_rows_tnmagnitude_kernel(tc, x, w1, w2, th, dx, og, base, out):
         for g in range(G):
             copy_part(scopy, 0, g, 1)
         square_part(0, 0)
-        square_part(0, 1)
-        interleave(vcopy, x_op[1])
         interleave(vcopy, dx_op[0])
-        quantize(x_op[1])
+        interleave(vcopy, x_op[1])
         quantize(dx_op[0])
-        products(z_bank, x_op, 1, ALL)
+        quantize(x_op[1])
         products(tz_bank, dx_op, 0, ALL)
-        interleave(vcopy, x_op[2])
-
-        sum_squares(nc.gpsimd, 0, 0, G)
-        quantize(x_op[2])
+        products(z_bank, x_op, 1, ALL)
         for g in range(G):
-            multiply(0, g)
+            copy_z(scopy, 1, g)
+        square_part(0, 1)
+        square_copy(1, 0, G)
+        multiply(0, 0)
+        interleave(vcopy, x_op[2])
         interleave(vcopy, dx_op[1])
-        add_products(nc.gpsimd, 0, 0, G)
-        copy_z(scopy, 1, 0)
-        copy_z(scopy, 1, 1)
-        products(z_bank, x_op, 2, (0, 1))
-        copy_z(scopy, 1, 2)
-        square_z(1, 3)
+        quantize(x_op[2])
+        quantize(dx_op[1])
+        products(z_bank, x_op, 2, ALL)
+        products(tz_bank, dx_op, 1, (0,))
+        multiply(0, 1)
+        products(tz_bank, dx_op, 1, (1,))
+        interleave(vcopy, dx_op[2])
+        sum_squares(nc.gpsimd, 0, 0, G)
+        sum_squares(nc.gpsimd, 1, 0, G)
+        for g in range(2, G):
+            multiply(0, g)
+            products(tz_bank, dx_op, 1, (g,))
+        for g in range(G):
+            square_z(2, g)
+        copy_z(scopy, 2, 3)
+        for g in range(3):
+            multiply(1, g)
         copy_z(vcopy, 2, 0)
         copy_z(vcopy, 2, 1)
-        copy_z(vcopy, 1, 3)
-        products(z_bank, x_op, 2, (2, 3))
-        quantize(dx_op[1])
-        products(tz_bank, dx_op, 1, ALL)
-        interleave(vcopy, dx_op[2])
-        square_copy(1, 0, 3)
-        square_copy(2, 0, 2)
-        square_z(2, 2)
-        square_z(2, 3)
-        sum_squares(nc.vector, 1, 0, G)
+        sum_squares(nc.vector, 2, 0, 2)
         quantize(dx_op[2])
-        sum_squares(nc.vector, 2, 0, G)
+        products(tz_bank, dx_op, 2, (0, 1, 2))
+        sum_squares(nc.vector, 2, 2, 4)
         nc.scalar.mul(out=th_bias[:], in_=th_sb[:], mul=-0.5)
         take_log(0, 0, G)
         take_log(1, 0, G)
         take_log(2, 0, G)
-        multiply(1, 0)
-        multiply(1, 1)
-        add_products(nc.gpsimd, 1, 0, 2)
-        products(tz_bank, dx_op, 2, (0, 1))
-        multiply(1, 2)
         multiply(1, 3)
-        products(tz_bank, dx_op, 2, (2, 3))
-        add_products(nc.gpsimd, 1, 2, 4)
+        products(tz_bank, dx_op, 2, (3,))
+        add_products(nc.gpsimd, 0, 256, 0, G)
         copy_z(vcopy, 2, 2)
-        copy_z(vcopy, 2, 3)
         multiply(2, 0)
         multiply(2, 1)
         multiply(2, 2)
         multiply(2, 3)
-        add_products(nc.vector, 2, 0, 2)
+        add_products(nc.vector, 256, 512, 0, 2)
+        add_products(nc.vector, 256, 512, 2, 3)
 
-        pieces = [(0, 0, 256), (0, 256, 256), (1, 0, 256), (1, 256, 256), (2, 0, 512), (3, 0, 384), (3, 384, 128)]
+        pieces = [(0, 0, 192), (0, 192, 320), (1, 0, 256), (1, 256, 256), (2, 0, 512), (3, 0, 384), (3, 384, 128)]
         scaled = {}
 
         def gate(i):
@@ -238,7 +235,7 @@ def tile_rows_tnmagnitude_kernel(tc, x, w1, w2, th, dx, og, base, out):
             if i > 0:
                 finish(i - 1)
             else:
-                add_products(nc.vector, 2, 2, 4)
+                add_products(nc.vector, 256, 512, 3, 4)
             nc.vector.scalar_tensor_tensor(
                 out=scaled[i][:], in0=gated[:], scalar=og_sb[:, g : g + 1], in1=slope[:], op0=ALU.mult, op1=ALU.mult
             )

from contextlib import ExitStack

import concourse.mybir as mybir

G, D, M, N = 4, 128, 128, 512
FLOPS = 4 * 2 * G * D * M * N

F32 = mybir.dt.float32
BF16 = mybir.dt.bfloat16
U32 = mybir.dt.uint32
U8 = mybir.dt.uint8
FP8X4 = mybir.dt.float8_e4m3fn_x4
ACT = mybir.ActivationFunctionType
ALU = mybir.AluOpType

P = 128
PACK = 4
ROWS = D // PACK
MM_N = 128
FLOOR = 0.05
CHUNKS = [(0, 128), (128, 128), (256, 256)]
BANK_COLS = 256


def tile_rows_tnmagnitude_kernel(tc, x, w1, w2, th, dx, og, base, out):
    nc = tc.nc
    with ExitStack() as ctx:
        sb = ctx.enter_context(tc.tile_pool(name="sb", bufs=1))
        ps = ctx.enter_context(tc.psum_pool(name="ps", bufs=1))
        ctx.enter_context(tc.manual_schedule())

        def operand(name, width):
            raw = sb.tile([P, PACK, width], F32, name=name + "_raw")
            packed = sb.tile([P, width * PACK], BF16, name=name + "_bf", align_bytes=64)
            codes = sb.tile([P, width], U32, name=name + "_codes", align_bytes=64)
            scales = sb.tile([P, width], U8, name=name + "_scales", align_bytes=64)
            return raw, packed, codes, scales

        w_op = [operand("w%d" % i, M) for i in range(2)]
        x_op = [operand("x%d" % c, CHUNKS[c][1]) for c in range(len(CHUNKS))]
        dx_op = [operand("dx%d" % c, CHUNKS[c][1]) for c in range(len(CHUNKS))]

        def load(op, src, c0, width):
            nc.sync.dma_start(out=op[0][:], in_=src.rearrange("g (p j) n -> (g p) j n", j=PACK)[:, :, c0 : c0 + width])

        base_sb = sb.tile([P, G, N], F32, name="base_sb")
        th_sb = sb.tile([P, G], F32, name="th_sb")
        og_sb = sb.tile([P, G], F32, name="og_sb")
        load(w_op[0], w1, 0, M)
        load(x_op[0], x, *CHUNKS[0])
        load(w_op[1], w2, 0, M)
        load(dx_op[0], dx, *CHUNKS[0])
        load(x_op[1], x, *CHUNKS[1])
        load(x_op[2], x, *CHUNKS[2])
        load(dx_op[1], dx, *CHUNKS[1])
        load(dx_op[2], dx, *CHUNKS[2])
        nc.sync.dma_start(out=base_sb[:], in_=base.rearrange("g m n -> m g n"))
        with nc.allow_non_contiguous_dma(reason="one value a partition and group"):
            nc.sync.dma_start(out=th_sb[:], in_=th.rearrange("g m o -> m (g o)"))
            nc.sync.dma_start(out=og_sb[:], in_=og.rearrange("g m o -> m (g o)"))

        two = sb.tile([P, 1], F32, name="two")
        ln2 = sb.tile([P, 1], F32, name="ln2")
        nc.gpsimd.memset(two[:], 2.0)
        nc.scalar.activation(out=ln2[:], in_=two[:], func=ACT.Ln)
        floor = sb.tile([P, 1], F32, name="floor")
        nc.scalar.mul(out=floor[:], in_=two[:], mul=FLOOR / 2.0)
        th_bias = sb.tile([P, G], F32, name="th_bias")

        def interleave(copy, op):
            copy(
                out=op[1][:].rearrange("p (c i t) -> p c t i", i=4, t=PACK),
                in_=op[0][:].rearrange("p t (c i) -> p c t i", i=4),
            )

        def quantize(op):
            nc.vector.quantize_mx(out=op[2][:].bitcast(FP8X4), scales=op[3][:], in_=op[1][:])

        z_bank = [ps.tile([P, 2, BANK_COLS], F32, name="z_bank%d" % g) for g in range(G)]
        tz_bank = [ps.tile([P, 2, BANK_COLS], F32, name="tz_bank%d" % g) for g in range(G)]

        def products(bank, op, c, groups, parts=(0, 1)):
            for part in parts:
                for c0 in range(0, CHUNKS[c][1], MM_N):
                    cols = slice(c0, c0 + MM_N)
                    for g in groups:
                        rows = slice(ROWS * g, ROWS * (g + 1))
                        nc.tensor.matmul_mx(
                            out=bank[g][:, part, cols],
                            lhsT=w_op[part][2][rows, :].bitcast(FP8X4),
                            lhsT_scale=w_op[part][3][rows, :],
                            rhs=op[c][2][rows, cols].bitcast(FP8X4),
                            rhs_scale=op[c][3][rows, cols],
                            start=True,
                            stop=True,
                        )

        nch = len(CHUNKS)
        z = [sb.tile([P, G, 2, CHUNKS[c][1]], F32, name="z%d" % c) for c in range(nch)]
        zsq = [sb.tile([P, G, 2, CHUNKS[c][1]], F32, name="zsq%d" % c) for c in range(nch)]
        prod = sb.tile([P, G, 2, N], F32, name="prod")
        ssum = [sb.tile([P, G, CHUNKS[c][1]], F32, name="ssum%d" % c) for c in range(nch)]
        logs = sb.tile([P, G, N], F32, name="logs")
        dot = sb.tile([P, G, N], F32, name="dot")
        vcopy = nc.vector.tensor_copy
        scopy = nc.scalar.copy

        def span(c):
            return slice(CHUNKS[c][0], CHUNKS[c][0] + CHUNKS[c][1])

        def copy_z(copy, c, g):
            copy(out=z[c][:, g, :, :], in_=z_bank[g][:, :, : CHUNKS[c][1]])

        def copy_part(copy, c, g, part):
            copy(out=z[c][:, g, part, :], in_=z_bank[g][:, part, : CHUNKS[c][1]])

        def square_z(c, g):
            nc.scalar.activation(out=zsq[c][:, g, :, :], in_=z_bank[g][:, :, : CHUNKS[c][1]], func=ACT.Square)

        def square_copy(c, g0, g1):
            nc.scalar.activation(out=zsq[c][:, g0:g1, :, :], in_=z[c][:, g0:g1, :, :], func=ACT.Square)

        def square_part(c, part):
            nc.scalar.activation(out=zsq[c][:, :, part, :], in_=z[c][:, :, part, :], func=ACT.Square)

        def sum_squares(eng, c, g0, g1):
            eng.tensor_tensor(out=ssum[c][:, g0:g1, :], in0=zsq[c][:, g0:g1, 0, :], in1=zsq[c][:, g0:g1, 1, :], op=ALU.add)

        def multiply(c, g):
            nc.vector.scalar_tensor_tensor(
                out=prod[:, g, :, span(c)], in0=tz_bank[g][:, :, : CHUNKS[c][1]], scalar=0.25, in1=z[c][:, g, :, :], op0=ALU.mult, op1=ALU.mult
            )

        def add_products(eng, c0, c1, g0, g1):
            eng.tensor_tensor(out=dot[:, g0:g1, c0:c1], in0=prod[:, g0:g1, 0, c0:c1], in1=prod[:, g0:g1, 1, c0:c1], op=ALU.add)

        def take_log(c, g0, g1):
            nc.scalar.activation(out=logs[:, g0:g1, span(c)], in_=ssum[c][:, g0:g1, :], func=ACT.Ln, bias=floor[:])

        ALL = range(G)
        interleave(vcopy, w_op[0])
        interleave(vcopy, x_op[0])
        quantize(w_op[0])
        quantize(x_op[0])
        products(z_bank, x_op, 0, ALL, (0,))
        for g in range(G):
            copy_part(scopy, 0, g, 0)
        interleave(vcopy, w_op[1])
        quantize(w_op[1])
        products(z_bank, x_op, 0, ALL, (1,))
        for g in range(G):
            copy_part(scopy, 0, g, 1)
        square_part(0, 0)
        interleave(vcopy, dx_op[0])
        interleave(vcopy, x_op[1])
        quantize(dx_op[0])
        quantize(x_op[1])
        products(tz_bank, dx_op, 0, ALL)
        products(z_bank, x_op, 1, ALL)
        for g in range(G):
            copy_z(scopy, 1, g)
        square_part(0, 1)
        square_copy(1, 0, G)
        multiply(0, 0)
        interleave(vcopy, x_op[2])
        interleave(vcopy, dx_op[1])
        quantize(x_op[2])
        quantize(dx_op[1])
        products(z_bank, x_op, 2, ALL)
        products(tz_bank, dx_op, 1, (0,))
        multiply(0, 1)
        products(tz_bank, dx_op, 1, (1,))
        interleave(vcopy, dx_op[2])
        sum_squares(nc.gpsimd, 0, 0, G)
        sum_squares(nc.gpsimd, 1, 0, G)
        for g in range(2, G):
            multiply(0, g)
            products(tz_bank, dx_op, 1, (g,))
        for g in range(G):
            square_z(2, g)
        copy_z(scopy, 2, 3)
        for g in range(3):
            multiply(1, g)
        copy_z(vcopy, 2, 0)
        copy_z(vcopy, 2, 1)
        sum_squares(nc.vector, 2, 0, 2)
        quantize(dx_op[2])
        products(tz_bank, dx_op, 2, (0, 1, 2))
        sum_squares(nc.vector, 2, 2, 4)
        nc.scalar.mul(out=th_bias[:], in_=th_sb[:], mul=-0.5)
        take_log(0, 0, G)
        take_log(1, 0, G)
        take_log(2, 0, G)
        multiply(1, 3)
        products(tz_bank, dx_op, 2, (3,))
        add_products(nc.gpsimd, 0, 256, 0, G)
        copy_z(vcopy, 2, 2)
        multiply(2, 0)
        multiply(2, 1)
        multiply(2, 2)
        multiply(2, 3)
        add_products(nc.vector, 256, 512, 0, 2)
        add_products(nc.vector, 256, 512, 2, 3)

        pieces = [(0, 0, 192), (0, 192, 320), (1, 0, 256), (1, 256, 256), (2, 0, 512), (3, 0, 384), (3, 384, 128)]
        scaled = {}

        def gate(i):
            g, c0, width = pieces[i]
            cols = slice(c0, c0 + width)
            mag = sb.tile([P, width], F32, name="mag%d" % i)
            inv2 = sb.tile([P, width], F32, name="inv2_%d" % i)
            tnh = sb.tile([P, width], F32, name="tnh%d" % i)
            nc.scalar.activation(out=mag[:], in_=logs[:, g, cols], func=ACT.Exp, scale=0.5)
            nc.scalar.activation(out=inv2[:], in_=logs[:, g, cols], func=ACT.Exp, scale=-0.5, bias=ln2[:])
            nc.scalar.activation(out=tnh[:], in_=mag[:], func=ACT.Tanh, scale=0.5, bias=th_bias[:, g : g + 1])
            return inv2, tnh

        def finish(i):
            g, c0, width = pieces[i]
            cols = slice(c0, c0 + width)
            res = sb.tile([P, width], F32, name="res%d" % i)
            nc.vector.tensor_tensor(out=res[:], in0=scaled[i][:], in1=base_sb[:, g, cols], op=ALU.add)
            nc.sync.dma_start(out=out[g, :, cols], in_=res[:])

        for i in range(len(pieces)):
            g, c0, width = pieces[i]
            cols = slice(c0, c0 + width)
            inv2, tnh = gate(i)
            slope = sb.tile([P, width], F32, name="slope%d" % i)
            gated = sb.tile([P, width], F32, name="gated%d" % i)
            scaled[i] = sb.tile([P, width], F32, name="scaled%d" % i)
            nc.vector.scalar_tensor_tensor(out=slope[:], in0=inv2[:], scalar=1.0, in1=tnh[:], op0=ALU.add, op1=ALU.subtract)
            nc.vector.scalar_tensor_tensor(out=gated[:], in0=tnh[:], scalar=1.0, in1=dot[:, g, cols], op0=ALU.add, op1=ALU.mult)
            if i > 0:
                finish(i - 1)
            else:
                add_products(nc.vector, 256, 512, 3, 4)
            nc.vector.scalar_tensor_tensor(
                out=scaled[i][:], in0=gated[:], scalar=og_sb[:, g : g + 1], in1=slope[:], op0=ALU.mult, op1=ALU.mult
            )
        finish(len(pieces) - 1)
